import numpy as np
CORES = [33,161,289,417,57,185,313,441]
N = 8
TK = 64
def setup_inputs(rng):
    return {"b": rng.standard_normal((N, 128, TK), dtype=np.float32), "l": (rng.standard_normal((N, 128, N * 128), dtype=np.float32) / 16)}
def setup_inputs_big(rng):
    d = setup_inputs(rng)
    for k in ("b",): d[k] = (d[k].astype(np.float32) * 1048576.0).astype(d[k].dtype)
    return d
def setup_inputs_small(rng):
    d = setup_inputs(rng)
    for k in ("b",): d[k] = (d[k].astype(np.float32) * (1 / 1048576.0)).astype(d[k].dtype)
    return d
def setup_inputs_apart(rng):
    d = setup_inputs(rng)
    f = (10.0 ** rng.permutation(np.linspace(-1.5, 1.5, N))).astype(np.float32).reshape(N, 1, 1)
    for k in ("b",): d[k] = (d[k].astype(np.float32) * f).astype(d[k].dtype)
    return d
def reference(b, l):
    B, L = b.astype(np.float64), l.astype(np.float64)
    y = np.zeros((N, 128, TK))
    for r in range(N):
        acc = B[r].copy()
        for s in range(r):
            acc -= L[r][:, 128 * s:128 * s + 128].T @ y[s]
        y[r] = acc
    return {"y": y.astype(np.float32)}

@@ -1,0 +1,191 @@
+from concourse.mybir import AluOpType
+
+N, TK, P = 8, 64, 128
+
+
+def _off(q):
+    return TK * q + P * (q * (q - 1) // 2)
+
+
+SCRATCH = {
+    "w": ("sbuf", [P, _off(N)], "float32"),
+    "yy": ("sbuf", [P, TK * N], "float32"),
+}
+for _q in range(1, N):
+    SCRATCH["ps%d" % _q] = ("psum", [P, 512], "float32")
+
+SEMAPHORES = (["r%d" % q for q in range(N - 1)] + ["m%d" % q for q in range(1, N)] + ["v%d" % q for q in range(1, N)]
+              + ["ldb", "ldl", "st", "sent"])
+
+ARRIVE = {1: [0], 2: [0, 1], 3: [0, 2, 1], 4: [0, 1, 2, 3], 5: [0, 1, 2, 4, 3], 6: [0, 1, 2, 5, 3, 4],
+          7: [0, 1, 2, 4, 6, 3, 5]}
+
+_CACHE = {}
+
+
+def _bits(m):
+    return bin(m).count("1")
+
+
+def _plan(T, topo):
+    if "p" in _CACHE:
+        return _CACHE["p"]
+    cores = list(T.cores)
+    world = range((max(topo.host(c) for c in cores) + 1) * topo.CORES_PER_HOST)
+    rk = lambda c: topo.rack(topo.host(c))
+    same_chip = lambda a, b: topo.host(a) == topo.host(b) and topo.chip(a) == topo.chip(b)
+
+    helper = {}
+    for q in range(N - 1):
+        o = cores[q]
+        far = [c for c in cores[q + 1:] if topo.host(c) == topo.host(o) and not topo.may_write(o, c)]
+        if far:
+            cand = [c for c in world if same_chip(c, o) and c not in cores and all(topo.may_write(c, f) for f in far)]
+            other = [c for c in cand if topo.die(c) != topo.die(o)]
+            helper[q] = (other or cand)[0]
+
+    hops = []
+    for q in range(N - 1):
+        o = cores[q]
+        direct = [c for c in cores[q + 1:] if topo.may_write(o, c)]
+        holders = list(direct)
+        if q in helper:
+            holders += [h for h in helper.values() if h == helper[q] or (rk(h) != rk(o) and topo.may_write(o, h))]
+        used = []
+        for c in cores[q + 1:]:
+            if c in direct:
+                hops.append((q, o, c))
+                continue
+            k = [h for h in holders if topo.may_write(h, c) and rk(h) == rk(c)][0]
+            hops.append((q, k, c))
+            if k not in direct and k not in used:
+                used.append(k)
+        for k in used:
+            hops.append((q, o, k))
+
+    onward = lambda q, c: len([1 for (q2, s, d) in hops if q2 == q and s == c])
+    rank_of = lambda c: cores.index(c) if c in cores else -1
+    sends, cnt = {}, {}
+    for s in sorted(set(h[1] for h in hops)):
+        mine = [h for h in hops if h[1] == s]
+        off_chip = [topo.mask(s, d) for (q, _, d) in mine if not same_chip(s, d)]
+        own = [h for h in mine if cores[h[0]] == s]
+        fwd = [h for h in mine if cores[h[0]] != s]
+        own.sort(key=lambda h: (-onward(h[0], h[2]), not same_chip(s, h[2]), -rank_of(h[2])))
+        fwd.sort(key=lambda h: (h[0], -rank_of(h[2])))
+        out = []
+        for (q, _, d) in own + fwd:
+            m = topo.mask(s, d)
+            if same_chip(s, d) and off_chip and (m & ~off_chip[0]):
+                m = m & ~off_chip[0]
+            out.append((q, d, m))
+            cnt[(d, q)] = _bits(m)
+        sends[s] = out
+    _CACHE["p"] = (sends, cnt)
+    return _CACHE["p"]
+
+
+def _schedule(r, order):
+    have, known, done, seq = {r}, set(), set(), []
+    left = {q: q for q in range(1, r + 1)}
+    state = {"new": None, "fill": 0}
+
+    def drain():
+        while True:
+            cand = sorted((q, s) for q in have for s in known if s < q and (q, s) not in done)
+            if not cand:
+                return
+            pick = cand[0]
+            if pick[1] == state["new"] and state["fill"] < 1:
+                rest = [c for c in cand if c[1] != state["new"]]
+                if rest:
+                    pick = rest[0]
+                    state["fill"] += 1
+            q, s = pick
+            done.add(pick)
+            seq.append(("mm", q, s, left[q] == q, left[q] == 1))
+            left[q] -= 1
+            if left[q] == 0:
+                seq.append(("vec", q))
+                known.add(q)
+                state["new"], state["fill"] = q, 0
+
+    for a in order:
+        if a == 0:
+            known.add(0)
+        else:
+            have.add(a)
+        drain()
+    return seq
+
+
+def rank_program(g, core, T, topo):
+    sends, cnt = _plan(T, topo)
+    mine = sends.get(core, [])
+    rank = T.rank_of(core)
+    if rank is None and not mine:
+        return
+    S, W, Y = T.sem, T.w, T.yy
+
+    if rank is not None:
+        o = _off(rank)
+        g.scalar.dma_start(W[:, o:o + TK], T.b[:]).then_inc(S.ldb, 16)
+        if rank > 0:
+            g.sync.dma_start(W[:, o + TK:_off(rank + 1)], T.l[:, 0:P * rank]).then_inc(S.ldl, 16)
+        else:
+            g.sync.dma_start(T.y[:], T.b[:]).then_inc(S.st, 16)
+            g.sync.wait_ge(S.st, 16)
+
+    total, seen = 0, set()
+    for (q, dst, mask) in mine:
+        if q not in seen:
+            seen.add(q)
+            if q == rank:
+                g.wait_ge(S.ldb, 16)
+                if rank > 0:
+                    g.wait_ge(S.ldl, 16)
+            else:
+                g.wait_ge(S["r%d" % q], cnt[(core, q)])
+        rid, pid = topo.addr(dst, core)
+        piece = W[:, _off(q):_off(q + 1)]
+        g.remote_dma(out_ap=piece, in_ap=piece, remote_sem=S["r%d" % q], local_sem=S.sent, pid=pid, routing_id=rid,
+                     dma_engine_mask=mask)
+        total += _bits(mask)
+    if total:
+        g.wait_ge(S.sent, total)
+    if not rank:
+        return
+
+    pe, ve = set(), set()
+
+    def need(queue, seen_set, key):
+        if key in seen_set:
+            return
+        seen_set.add(key)
+        kind, q = key
+        if kind == "y":
+            queue.wait_ge(S["v%d" % q], 1)
+        elif q != rank:
+            queue.wait_ge(S["r%d" % q], cnt[(core, q)])
+        else:
+            queue.wait_ge(S.ldl if kind == "tiles" else S.ldb, 16)
+
+    for it in _schedule(rank, ARRIVE[rank]):
+        q = it[1]
+        o = _off(q)
+        acc = T["ps%d" % q][:, 0:TK]
+        if it[0] == "mm":
+            s = it[2]
+            need(g.tensor, pe, ("tiles", q))
+            need(g.tensor, pe, ("y", s) if s else ("tiles", 0))
+            rhs = Y[:, TK * s:TK * (s + 1)] if s else W[:, 0:TK]
+            g.tensor.matmul(acc, W[:, o + TK + P * s:o + TK + P * (s + 1)], rhs, it[3], it[4]).then_inc(S["m%d" % q], 1)
+        else:
+            g.vector.wait_ge(S["m%d" % q], q)
+            need(g.vector, ve, ("b", q))
+            g.vector.tensor_tensor(Y[:, TK * q:TK * (q + 1)], W[:, o:o + TK], acc,
+                                   AluOpType.subtract).then_inc(S["v%d" % q], 1)
+
+    g.sync.wait_ge(S["v%d" % rank], 1)
+    g.sync.dma_start(T.y[:], Y[:, TK * rank:TK * (rank + 1)]).then_inc(S.st, 16)
+    g.sync.wait_ge(S.st, 16)

@@ -14,8 +14,23 @@ SCRATCH = {
 for _q in range(1, N):
     SCRATCH["ps%d" % _q] = ("psum", [P, 512], "float32")
 
-SEMAPHORES = (["r%d" % q for q in range(N - 1)] + ["m%d" % q for q in range(1, N)] + ["v%d" % q for q in range(1, N)]
-              + ["ldb", "ldl", "st", "sent"])
+SPLIT = {3: 1, 4: 2, 5: 2, 6: 3}
+
+
+def _chunks(q):
+    a, z = _off(q), _off(q + 1)
+    if q in SPLIT:
+        mid = a + TK + P * SPLIT[q]
+        return [(a, mid), (mid, z)]
+    return [(a, z)]
+
+
+def _chunk_of(q, s):
+    return 1 if q in SPLIT and s >= SPLIT[q] else 0
+
+
+SEMAPHORES = (["r%d_%d" % (q, k) for q in range(N - 1) for k in range(len(_chunks(q)))] + ["m%d" % q for q in range(1, N)]
+              + ["v%d" % q for q in range(1, N)] + ["ldb", "ld0", "ld1", "st", "sent"])
 
 ARRIVE = {1: [0], 2: [0, 1], 3: [0, 2, 1], 4: [0, 1, 2, 3], 5: [0, 1, 2, 4, 3], 6: [0, 1, 2, 5, 3, 4],
           7: [0, 1, 2, 4, 6, 3, 5]}
@@ -74,11 +89,13 @@ def _plan(T, topo):
         own.sort(key=lambda h: (-onward(h[0], h[2]), not same_chip(s, h[2]), -rank_of(h[2])))
         fwd.sort(key=lambda h: (h[0], -rank_of(h[2])))
         out = []
-        for (q, _, d) in own + fwd:
+        steps = [(h, k) for k in range(2) for h in own if k < len(_chunks(h[0]))]
+        steps += [(h, k) for q in sorted(set(h[0] for h in fwd)) for k in range(len(_chunks(q))) for h in fwd if h[0] == q]
+        for ((q, _, d), k) in steps:
             m = topo.mask(s, d)
             if same_chip(s, d) and off_chip and (m & ~off_chip[0]):
                 m = m & ~off_chip[0]
-            out.append((q, d, m))
+            out.append((q, k, d, m))
             cnt[(d, q)] = _bits(m)
         sends[s] = out
     _CACHE["p"] = (sends, cnt)
@@ -86,13 +103,14 @@ def _plan(T, topo):
 
 
 def _schedule(r, order):
-    have, known, done, seq = {r}, set(), set(), []
+    have, known, done, seq = set((r, k) for k in range(2)), set(), set(), []
     left = {q: q for q in range(1, r + 1)}
     state = {"new": None, "fill": 0}
 
     def drain():
         while True:
-            cand = sorted((q, s) for q in have for s in known if s < q and (q, s) not in done)
+            cand = sorted((q, s) for q in range(1, r + 1) for s in known
+                          if s < q and (q, _chunk_of(q, s)) in have and (q, s) not in done)
             if not cand:
                 return
             pick = cand[0]
@@ -111,11 +129,12 @@ def _schedule(r, order):
                 state["new"], state["fill"] = q, 0
 
     for a in order:
-        if a == 0:
-            known.add(0)
-        else:
-            have.add(a)
-        drain()
+        for k in range(len(_chunks(a))):
+            if a == 0:
+                known.add(0)
+            else:
+                have.add((a, k))
+            drain()
     return seq
 
 
@@ -130,26 +149,29 @@ def rank_program(g, core, T, topo):
     if rank is not None:
         o = _off(rank)
         g.scalar.dma_start(W[:, o:o + TK], T.b[:]).then_inc(S.ldb, 16)
-        if rank > 0:
-            g.sync.dma_start(W[:, o + TK:_off(rank + 1)], T.l[:, 0:P * rank]).then_inc(S.ldl, 16)
-        else:
+        for k, (a, z) in enumerate(_chunks(rank)):
+            a = max(a, o + TK)
+            if z > a:
+                g.sync.dma_start(W[:, a:z], T.l[:, a - o - TK:z - o - TK]).then_inc(S["ld%d" % k], 16)
+        if rank == 0:
             g.sync.dma_start(T.y[:], T.b[:]).then_inc(S.st, 16)
             g.sync.wait_ge(S.st, 16)
 
     total, seen = 0, set()
-    for (q, dst, mask) in mine:
-        if q not in seen:
-            seen.add(q)
+    for (q, k, dst, mask) in mine:
+        if (q, k) not in seen:
+            seen.add((q, k))
             if q == rank:
-                g.wait_ge(S.ldb, 16)
+                if k == 0:
+                    g.wait_ge(S.ldb, 16)
                 if rank > 0:
-                    g.wait_ge(S.ldl, 16)
+                    g.wait_ge(S["ld%d" % k], 16)
             else:
-                g.wait_ge(S["r%d" % q], cnt[(core, q)])
+                g.wait_ge(S["r%d_%d" % (q, k)], cnt[(core, q)])
         rid, pid = topo.addr(dst, core)
-        piece = W[:, _off(q):_off(q + 1)]
-        g.remote_dma(out_ap=piece, in_ap=piece, remote_sem=S["r%d" % q], local_sem=S.sent, pid=pid, routing_id=rid,
-                     dma_engine_mask=mask)
+        a, z = _chunks(q)[k]
+        g.remote_dma(out_ap=W[:, a:z], in_ap=W[:, a:z], remote_sem=S["r%d_%d" % (q, k)], local_sem=S.sent, pid=pid,
+                     routing_id=rid, dma_engine_mask=mask)
         total += _bits(mask)
     if total:
         g.wait_ge(S.sent, total)
@@ -162,13 +184,13 @@ def rank_program(g, core, T, topo):
         if key in seen_set:
             return
         seen_set.add(key)
-        kind, q = key
+        kind, q, k = key
         if kind == "y":
             queue.wait_ge(S["v%d" % q], 1)
         elif q != rank:
-            queue.wait_ge(S["r%d" % q], cnt[(core, q)])
+            queue.wait_ge(S["r%d_%d" % (q, k)], cnt[(core, q)])
         else:
-            queue.wait_ge(S.ldl if kind == "tiles" else S.ldb, 16)
+            queue.wait_ge(S["ld%d" % k] if kind == "tiles" else S.ldb, 16)
 
     for it in _schedule(rank, ARRIVE[rank]):
         q = it[1]
@@ -176,13 +198,13 @@ def rank_program(g, core, T, topo):
         acc = T["ps%d" % q][:, 0:TK]
         if it[0] == "mm":
             s = it[2]
-            need(g.tensor, pe, ("tiles", q))
-            need(g.tensor, pe, ("y", s) if s else ("tiles", 0))
+            need(g.tensor, pe, ("tiles", q, _chunk_of(q, s)))
+            need(g.tensor, pe, ("y", s, 0) if s else ("tiles", 0, 0))
             rhs = Y[:, TK * s:TK * (s + 1)] if s else W[:, 0:TK]
             g.tensor.matmul(acc, W[:, o + TK + P * s:o + TK + P * (s + 1)], rhs, it[3], it[4]).then_inc(S["m%d" % q], 1)
         else:
             g.vector.wait_ge(S["m%d" % q], q)
-            need(g.vector, ve, ("b", q))
+            need(g.vector, ve, ("b", q, 0))
             g.vector.tensor_tensor(Y[:, TK * q:TK * (q + 1)], W[:, o:o + TK], acc,
                                    AluOpType.subtract).then_inc(S["v%d" % q], 1)
 

@@ -14,26 +14,31 @@ SCRATCH = {
 for _q in range(1, N):
     SCRATCH["ps%d" % _q] = ("psum", [P, 512], "float32")
 
-SPLIT = {3: 1, 4: 2, 5: 2, 6: 3}
+TILES = {0: [0], 1: [0, 1], 2: [0, 2], 3: [0, 1, 2], 4: [0, 2, 2], 5: [1, 1, 2, 1], 6: [3, 3], 7: [7]}
+ENTRY = [5]
 
 
 def _chunks(q):
-    a, z = _off(q), _off(q + 1)
-    if q in SPLIT:
-        mid = a + TK + P * SPLIT[q]
-        return [(a, mid), (mid, z)]
-    return [(a, z)]
+    out, a = [], _off(q)
+    for k, n in enumerate(TILES[q]):
+        z = a + P * n + (TK if k == 0 else 0)
+        out.append((a, z))
+        a = z
+    return out
 
 
 def _chunk_of(q, s):
-    return 1 if q in SPLIT and s >= SPLIT[q] else 0
+    k = 0
+    while s >= sum(TILES[q][:k + 1]):
+        k += 1
+    return k
 
 
 SEMAPHORES = (["r%d_%d" % (q, k) for q in range(N - 1) for k in range(len(_chunks(q)))] + ["m%d" % q for q in range(1, N)]
-              + ["v%d" % q for q in range(1, N)] + ["ldb", "ld0", "ld1", "st", "sent"])
+              + ["v%d" % q for q in range(1, N)] + ["ldb", "ld0", "ld1", "ld2", "ld3", "st", "sent"])
 
 ARRIVE = {1: [0], 2: [0, 1], 3: [0, 2, 1], 4: [0, 1, 2, 3], 5: [0, 1, 2, 4, 3], 6: [0, 1, 2, 5, 3, 4],
-          7: [0, 1, 2, 4, 6, 3, 5]}
+          7: [0, 1, 2, 4, 6, (5, 0), (5, 1), 3, (5, 2), (5, 3)]}
 
 _CACHE = {}
 
@@ -50,60 +55,75 @@ def _plan(T, topo):
     rk = lambda c: topo.rack(topo.host(c))
     same_chip = lambda a, b: topo.host(a) == topo.host(b) and topo.chip(a) == topo.chip(b)
 
-    helper = {}
+    gate = {}
     for q in range(N - 1):
         o = cores[q]
         far = [c for c in cores[q + 1:] if topo.host(c) == topo.host(o) and not topo.may_write(o, c)]
         if far:
             cand = [c for c in world if same_chip(c, o) and c not in cores and all(topo.may_write(c, f) for f in far)]
             other = [c for c in cand if topo.die(c) != topo.die(o)]
-            helper[q] = (other or cand)[0]
+            gate[q] = (other if len(other) >= 2 else cand)[:2]
+    gates_of = {q: [j for j in gate if j == q or (rk(gate[j][0]) != rk(cores[q]) and topo.may_write(cores[q], gate[j][0]))]
+                for q in gate}
+    served = {j: [q for q in gate if j in gates_of[q]] for j in gate}
+
+    def side(q, k, j):
+        i = 1 if q == min(served[j]) or (len(TILES[q]) == 3 and k == 1) else 0
+        return gate[j][min(i, len(gate[j]) - 1)]
 
     hops = []
     for q in range(N - 1):
         o = cores[q]
         direct = [c for c in cores[q + 1:] if topo.may_write(o, c)]
-        holders = list(direct)
-        if q in helper:
-            holders += [h for h in helper.values() if h == helper[q] or (rk(h) != rk(o) and topo.may_write(o, h))]
-        used = []
-        for c in cores[q + 1:]:
-            if c in direct:
-                hops.append((q, o, c))
-                continue
-            k = [h for h in holders if topo.may_write(h, c) and rk(h) == rk(c)][0]
-            hops.append((q, k, c))
-            if k not in direct and k not in used:
-                used.append(k)
-        for k in used:
-            hops.append((q, o, k))
+        pair, via = [], []
+        if q in ENTRY:
+            r = [h for h in direct for c in cores[q + 1:] if c not in direct and topo.may_write(h, c) and rk(h) == rk(c)][0]
+            via = [c for c in cores[q + 1:] if rk(c) == rk(r)]
+            cand = [c for c in world if same_chip(c, r) and c not in cores and topo.may_write(o, c)
+                    and all(topo.may_write(c, v) for v in via)]
+            pair = [[c for c in cand if topo.die(c) == topo.die(r)][0], [c for c in cand if topo.die(c) != topo.die(r)][0]]
+        for k in range(len(TILES[q])):
+            used = []
+            for c in cores[q + 1:]:
+                if c in via:
+                    relay = [pair[k % 2]]
+                elif c in direct:
+                    hops.append((q, k, o, c))
+                    continue
+                else:
+                    relay = [h for h in direct if topo.may_write(h, c) and rk(h) == rk(c)]
+                    if not relay:
+                        relay = [side(q, k, j) for j in gates_of[q] if rk(gate[j][0]) == rk(c)]
+                hops.append((q, k, relay[0], c))
+                if relay[0] not in cores and relay[0] not in used:
+                    used.append(relay[0])
+            for h in used:
+                hops.append((q, k, o, h))
 
-    onward = lambda q, c: len([1 for (q2, s, d) in hops if q2 == q and s == c])
+    onward = lambda h: len([1 for x in hops if x[:2] == h[:2] and x[2] == h[3]])
     rank_of = lambda c: cores.index(c) if c in cores else -1
     sends, cnt = {}, {}
-    for s in sorted(set(h[1] for h in hops)):
-        mine = [h for h in hops if h[1] == s]
-        off_chip = [topo.mask(s, d) for (q, _, d) in mine if not same_chip(s, d)]
+    for s in sorted(set(h[2] for h in hops)):
+        mine = [h for h in hops if h[2] == s]
+        off_chip = [topo.mask(s, h[3]) for h in mine if not same_chip(s, h[3])]
         own = [h for h in mine if cores[h[0]] == s]
         fwd = [h for h in mine if cores[h[0]] != s]
-        own.sort(key=lambda h: (-onward(h[0], h[2]), not same_chip(s, h[2]), -rank_of(h[2])))
-        fwd.sort(key=lambda h: (h[0], -rank_of(h[2])))
+        own.sort(key=lambda h: (onward(h) == 0, h[3] in cores, h[1], not same_chip(s, h[3]), -rank_of(h[3])))
+        fwd.sort(key=lambda h: (h[0], h[1], -rank_of(h[3])))
         out = []
-        steps = [(h, k) for k in range(2) for h in own if k < len(_chunks(h[0]))]
-        steps += [(h, k) for q in sorted(set(h[0] for h in fwd)) for k in range(len(_chunks(q))) for h in fwd if h[0] == q]
-        for ((q, _, d), k) in steps:
+        for (q, k, _, d) in own + fwd:
             m = topo.mask(s, d)
             if same_chip(s, d) and off_chip and (m & ~off_chip[0]):
                 m = m & ~off_chip[0]
             out.append((q, k, d, m))
-            cnt[(d, q)] = _bits(m)
+            cnt[(d, q, k)] = _bits(m)
         sends[s] = out
     _CACHE["p"] = (sends, cnt)
     return _CACHE["p"]
 
 
 def _schedule(r, order):
-    have, known, done, seq = set((r, k) for k in range(2)), set(), set(), []
+    have, known, done, seq = set((r, k) for k in range(len(TILES[r]))), set(), set(), []
     left = {q: q for q in range(1, r + 1)}
     state = {"new": None, "fill": 0}
 
@@ -129,11 +149,11 @@ def _schedule(r, order):
                 state["new"], state["fill"] = q, 0
 
     for a in order:
-        for k in range(len(_chunks(a))):
-            if a == 0:
+        for piece in ([a] if isinstance(a, tuple) else [(a, k) for k in range(len(TILES[a]))]):
+            if piece[0] == 0:
                 known.add(0)
             else:
-                have.add((a, k))
+                have.add(piece)
             drain()
     return seq
 
@@ -164,10 +184,10 @@ def rank_program(g, core, T, topo):
             if q == rank:
                 if k == 0:
                     g.wait_ge(S.ldb, 16)
-                if rank > 0:
+                if TILES[q][k]:
                     g.wait_ge(S["ld%d" % k], 16)
             else:
-                g.wait_ge(S["r%d_%d" % (q, k)], cnt[(core, q)])
+                g.wait_ge(S["r%d_%d" % (q, k)], cnt[(core, q, k)])
         rid, pid = topo.addr(dst, core)
         a, z = _chunks(q)[k]
         g.remote_dma(out_ap=W[:, a:z], in_ap=W[:, a:z], remote_sem=S["r%d_%d" % (q, k)], local_sem=S.sent, pid=pid,
@@ -188,7 +208,7 @@ def rank_program(g, core, T, topo):
         if kind == "y":
             queue.wait_ge(S["v%d" % q], 1)
         elif q != rank:
-            queue.wait_ge(S["r%d_%d" % (q, k)], cnt[(core, q)])
+            queue.wait_ge(S["r%d_%d" % (q, k)], cnt[(core, q, k)])
         else:
             queue.wait_ge(S["ld%d" % k] if kind == "tiles" else S.ldb, 16)
 

@@ -1,6 +1,7 @@
 from concourse.mybir import AluOpType
 
 N, TK, P = 8, 64, 128
+NL = 4
 
 
 def _off(q):
@@ -14,8 +15,10 @@ SCRATCH = {
 for _q in range(1, N):
     SCRATCH["ps%d" % _q] = ("psum", [P, 512], "float32")
 
-TILES = {0: [0], 1: [0, 1], 2: [0, 2], 3: [0, 1, 2], 4: [0, 2, 2], 5: [1, 1, 2, 1], 6: [3, 3], 7: [7]}
+TILES = {0: [0], 1: [0, 1], 2: [0, 2], 3: [0, 1, 2], 4: [0, 2, 1, 1], 5: [1, 1, 1, 1, 1], 6: [2, 1, 1, 1, 1], 7: [7]}
 ENTRY = [5]
+LAUNCH = {4: ({0: 0, 1: 0, 2: 0, 3: 0}, [5]), 5: ({3: 0, 4: 0}, None), 6: ({2: 0, 3: 1, 4: 0}, None)}
+PIECES = {7: [(1, 1), (2, 2), (3, 3)], 6: [(1, 1), (2, 2), (3, 3)], 5: [(1, 2), (3, 3)], 4: [(1, 3)]}
 
 
 def _chunks(q):
@@ -34,11 +37,10 @@ def _chunk_of(q, s):
     return k
 
 
-SEMAPHORES = (["r%d_%d" % (q, k) for q in range(N - 1) for k in range(len(_chunks(q)))] + ["m%d" % q for q in range(1, N)]
-              + ["v%d" % q for q in range(1, N)] + ["ldb", "ld0", "ld1", "ld2", "ld3", "st", "sent"])
-
-ARRIVE = {1: [0], 2: [0, 1], 3: [0, 2, 1], 4: [0, 1, 2, 3], 5: [0, 1, 2, 4, 3], 6: [0, 1, 2, 5, 3, 4],
-          7: [0, 1, 2, 4, 6, (5, 0), (5, 1), 3, (5, 2), (5, 3)]}
+_YS = sorted(set([p for u in PIECES for p in PIECES[u]] + [(q, q) for q in range(1, NL)]))
+SEMAPHORES = (["r%d_%d" % (q, k) for q in range(N - 1) for k in range(len(_chunks(q)))] + ["y%d_%d" % p for p in _YS]
+              + ["m%d" % q for q in range(1, N)] + ["v%d" % q for q in range(1, N)]
+              + ["ld%d" % k for k in range(max(len(t) for t in TILES.values()))] + ["ldb", "st", "sent"])
 
 _CACHE = {}
 
@@ -54,112 +56,116 @@ def _plan(T, topo):
     world = range((max(topo.host(c) for c in cores) + 1) * topo.CORES_PER_HOST)
     rk = lambda c: topo.rack(topo.host(c))
     same_chip = lambda a, b: topo.host(a) == topo.host(b) and topo.chip(a) == topo.chip(b)
+    low, up = list(range(NL)), list(range(NL, N))
 
-    gate = {}
-    for q in range(N - 1):
+    solver = {}
+    for q in low:
         o = cores[q]
-        far = [c for c in cores[q + 1:] if topo.host(c) == topo.host(o) and not topo.may_write(o, c)]
-        if far:
-            cand = [c for c in world if same_chip(c, o) and c not in cores and all(topo.may_write(c, f) for f in far)]
+        if rk(o) == rk(cores[N - 1]):
+            near = [cores[u] for u in up if rk(cores[u]) == rk(o)]
+            cand = [c for c in world if same_chip(c, o) and c not in cores and all(topo.may_write(c, n) for n in near)]
             other = [c for c in cand if topo.die(c) != topo.die(o)]
-            gate[q] = (other if len(other) >= 2 else cand)[:2]
-    gates_of = {q: [j for j in gate if j == q or (rk(gate[j][0]) != rk(cores[q]) and topo.may_write(cores[q], gate[j][0]))]
-                for q in gate}
-    served = {j: [q for q in gate if j in gates_of[q]] for j in gate}
-
-    def side(q, k, j):
-        i = 1 if q == min(served[j]) or (len(TILES[q]) == 3 and k == 1) else 0
-        return gate[j][min(i, len(gate[j]) - 1)]
+            solver[q] = (other or cand)[0]
+    sol = [solver[q] for q in sorted(solver)]
+    serve = {}
+    for u in up:
+        ok = [s for s in sol if topo.may_write(s, cores[u])]
+        home = [s for s in ok if topo.host(s) == topo.host(cores[u])]
+        serve[u] = (home or ok)[0]
 
     hops = []
-    for q in range(N - 1):
+    for q in low:
+        o = cores[q]
+        for k in range(len(TILES[q])):
+            for s in sol:
+                if topo.may_write(o, s):
+                    hops.append((q, k, o, s))
+                else:
+                    hops.append((q, k, [x for x in sol if topo.may_write(o, x) and topo.may_write(x, s)][0], s))
+    first = [s for s in sol if topo.may_write(cores[0], s)][0]
+    for u in up:
+        hops.append((0, 0, first if topo.may_write(first, cores[u]) else serve[u], cores[u]))
+    for q in low[1:]:
+        if q not in solver:
+            for p in range(q):
+                for k in range(len(TILES[p])):
+                    hops.append((p, k, cores[p], cores[q]))
+
+    for q in up[:-1]:
         o = cores[q]
         direct = [c for c in cores[q + 1:] if topo.may_write(o, c)]
-        pair, via = [], []
+        turn, via = [], []
         if q in ENTRY:
             r = [h for h in direct for c in cores[q + 1:] if c not in direct and topo.may_write(h, c) and rk(h) == rk(c)][0]
             via = [c for c in cores[q + 1:] if rk(c) == rk(r)]
             cand = [c for c in world if same_chip(c, r) and c not in cores and topo.may_write(o, c)
                     and all(topo.may_write(c, v) for v in via)]
-            pair = [[c for c in cand if topo.die(c) == topo.die(r)][0], [c for c in cand if topo.die(c) != topo.die(r)][0]]
+            here = [c for c in cand if topo.die(c) == topo.die(r)]
+            there = [c for c in cand if topo.die(c) != topo.die(r)]
+            turn = [here[0]] + [there[(k + 1) % 2] for k in range(1, len(TILES[q]))]
         for k in range(len(TILES[q])):
             used = []
             for c in cores[q + 1:]:
                 if c in via:
-                    relay = [pair[k % 2]]
+                    relay = turn[k]
                 elif c in direct:
                     hops.append((q, k, o, c))
                     continue
                 else:
-                    relay = [h for h in direct if topo.may_write(h, c) and rk(h) == rk(c)]
-                    if not relay:
-                        relay = [side(q, k, j) for j in gates_of[q] if rk(gate[j][0]) == rk(c)]
-                hops.append((q, k, relay[0], c))
-                if relay[0] not in cores and relay[0] not in used:
-                    used.append(relay[0])
+                    relay = [h for h in direct if topo.may_write(h, c) and rk(h) == rk(c)][0]
+                hops.append((q, k, relay, c))
+                if relay not in cores and relay not in used:
+                    used.append(relay)
             for h in used:
                 hops.append((q, k, o, h))
+
+    busy = set(c for h in hops for c in h[2:])
+    for q in sorted(LAUNCH):
+        o = cores[q]
+        which, only = LAUNCH[q]
+        free = [c for c in world if same_chip(c, o) and c not in cores and c not in busy and topo.die(c) == topo.die(o)]
+        free.reverse()
+        handed = []
+        for i, h in enumerate(hops):
+            if h[0] == q and h[2] == o and h[1] in which and (only is None or h[3] in [cores[u] for u in only]):
+                lc = free[which[h[1]]]
+                hops[i] = (q, h[1], lc, h[3])
+                if (h[1], lc) not in handed:
+                    handed.append((h[1], lc))
+        for (k, lc) in handed:
+            hops.append((q, k, o, lc))
+
+    ys = {}
+    for q in solver:
+        mine = sorted([u for u in up if serve[u] == solver[q]], reverse=True)
+        items = sorted((hi, i, lo, cores[u]) for i, u in enumerate(mine) for (lo, hi) in PIECES[u])
+        ys[solver[q]] = [(lo, hi, d) for (hi, i, lo, d) in items] + [(q, q, cores[q])]
 
     onward = lambda h: len([1 for x in hops if x[:2] == h[:2] and x[2] == h[3]])
     rank_of = lambda c: cores.index(c) if c in cores else -1
     sends, cnt = {}, {}
     for s in sorted(set(h[2] for h in hops)):
         mine = [h for h in hops if h[2] == s]
-        off_chip = [topo.mask(s, h[3]) for h in mine if not same_chip(s, h[3])]
+        dsts = [h[3] for h in mine] + [d for (_, _, d) in ys.get(s, [])]
+        off_chip = [topo.mask(s, d) for d in dsts if not same_chip(s, d)]
         own = [h for h in mine if cores[h[0]] == s]
         fwd = [h for h in mine if cores[h[0]] != s]
-        own.sort(key=lambda h: (onward(h) == 0, h[3] in cores, h[1], not same_chip(s, h[3]), -rank_of(h[3])))
-        fwd.sort(key=lambda h: (h[0], h[1], -rank_of(h[3])))
+        own.sort(key=lambda h: (h[1], onward(h) == 0, same_chip(s, h[3]), -rank_of(h[3])))
+        fwd.sort(key=lambda h: (h[3] not in sol, h[0], h[1], -rank_of(h[3])))
         out = []
-        for (q, k, _, d) in own + fwd:
+        for (kind, a, b, d) in [("r", h[0], h[1], h[3]) for h in own + fwd] + [("y", lo, hi, d) for (lo, hi, d) in ys.get(s, [])]:
             m = topo.mask(s, d)
             if same_chip(s, d) and off_chip and (m & ~off_chip[0]):
                 m = m & ~off_chip[0]
-            out.append((q, k, d, m))
-            cnt[(d, q, k)] = _bits(m)
+            out.append((kind, a, b, d, m))
+            cnt[(d, "%s%d_%d" % (kind, a, b))] = _bits(m)
         sends[s] = out
-    _CACHE["p"] = (sends, cnt)
+    _CACHE["p"] = (sends, cnt, solver)
     return _CACHE["p"]
 
 
-def _schedule(r, order):
-    have, known, done, seq = set((r, k) for k in range(len(TILES[r]))), set(), set(), []
-    left = {q: q for q in range(1, r + 1)}
-    state = {"new": None, "fill": 0}
-
-    def drain():
-        while True:
-            cand = sorted((q, s) for q in range(1, r + 1) for s in known
-                          if s < q and (q, _chunk_of(q, s)) in have and (q, s) not in done)
-            if not cand:
-                return
-            pick = cand[0]
-            if pick[1] == state["new"] and state["fill"] < 1:
-                rest = [c for c in cand if c[1] != state["new"]]
-                if rest:
-                    pick = rest[0]
-                    state["fill"] += 1
-            q, s = pick
-            done.add(pick)
-            seq.append(("mm", q, s, left[q] == q, left[q] == 1))
-            left[q] -= 1
-            if left[q] == 0:
-                seq.append(("vec", q))
-                known.add(q)
-                state["new"], state["fill"] = q, 0
-
-    for a in order:
-        for piece in ([a] if isinstance(a, tuple) else [(a, k) for k in range(len(TILES[a]))]):
-            if piece[0] == 0:
-                known.add(0)
-            else:
-                have.add(piece)
-            drain()
-    return seq
-
-
 def rank_program(g, core, T, topo):
-    sends, cnt = _plan(T, topo)
+    sends, cnt, solver = _plan(T, topo)
     mine = sends.get(core, [])
     rank = T.rank_of(core)
     if rank is None and not mine:
@@ -178,25 +184,47 @@ def rank_program(g, core, T, topo):
             g.sync.wait_ge(S.st, 16)
 
     total, seen = 0, set()
-    for (q, k, dst, mask) in mine:
-        if (q, k) not in seen:
-            seen.add((q, k))
-            if q == rank:
-                if k == 0:
-                    g.wait_ge(S.ldb, 16)
-                if TILES[q][k]:
-                    g.wait_ge(S["ld%d" % k], 16)
-            else:
-                g.wait_ge(S["r%d_%d" % (q, k)], cnt[(core, q, k)])
+    for (kind, a, b, dst, mask) in mine:
+        name = "%s%d_%d" % (kind, a, b)
+        if kind == "y":
+            for s in range(a, b + 1):
+                if ("v", s) not in seen:
+                    seen.add(("v", s))
+                    g.wait_ge(S["v%d" % s], 1)
+            buf, c0, c1 = Y, TK * a, TK * (b + 1)
+        else:
+            if name not in seen:
+                seen.add(name)
+                if a == rank:
+                    if b == 0:
+                        g.wait_ge(S.ldb, 16)
+                    if TILES[a][b]:
+                        g.wait_ge(S["ld%d" % b], 16)
+                else:
+                    g.wait_ge(S[name], cnt[(core, name)])
+            buf = W
+            c0, c1 = _chunks(a)[b]
         rid, pid = topo.addr(dst, core)
-        a, z = _chunks(q)[k]
-        g.remote_dma(out_ap=W[:, a:z], in_ap=W[:, a:z], remote_sem=S["r%d_%d" % (q, k)], local_sem=S.sent, pid=pid,
+        g.remote_dma(out_ap=buf[:, c0:c1], in_ap=buf[:, c0:c1], remote_sem=S[name], local_sem=S.sent, pid=pid,
                      routing_id=rid, dma_engine_mask=mask)
         total += _bits(mask)
     if total:
         g.wait_ge(S.sent, total)
-    if not rank:
+
+    if core in solver.values():
+        lo, hi, pieces = 1, NL - 1, []
+    elif not rank:
         return
+    elif rank in solver:
+        name = "y%d_%d" % (rank, rank)
+        g.sync.wait_ge(S[name], cnt[(core, name)])
+        g.sync.dma_start(T.y[:], Y[:, TK * rank:TK * (rank + 1)]).then_inc(S.st, 16)
+        g.sync.wait_ge(S.st, 16)
+        return
+    elif rank < NL:
+        lo, hi, pieces = 1, rank, []
+    else:
+        lo, hi, pieces = NL, rank, PIECES[rank]
 
     pe, ve = set(), set()
 
@@ -207,27 +235,33 @@ def rank_program(g, core, T, topo):
         kind, q, k = key
         if kind == "y":
             queue.wait_ge(S["v%d" % q], 1)
+        elif kind == "p":
+            queue.wait_ge(S["y%d_%d" % (q, k)], cnt[(core, "y%d_%d" % (q, k))])
         elif q != rank:
-            queue.wait_ge(S["r%d_%d" % (q, k)], cnt[(core, q, k)])
+            queue.wait_ge(S["r%d_%d" % (q, k)], cnt[(core, "r%d_%d" % (q, k))])
         else:
             queue.wait_ge(S["ld%d" % k] if kind == "tiles" else S.ldb, 16)
 
-    for it in _schedule(rank, ARRIVE[rank]):
-        q = it[1]
-        o = _off(q)
-        acc = T["ps%d" % q][:, 0:TK]
-        if it[0] == "mm":
-            s = it[2]
+    for s in range(hi):
+        for q in range(max(lo, s + 1), hi + 1):
+            o = _off(q)
+            acc = T["ps%d" % q][:, 0:TK]
+            if s == 0:
+                need(g.tensor, pe, ("tiles", 0, 0))
+            elif s < lo:
+                need(g.tensor, pe, ("p",) + [p for p in pieces if p[0] <= s <= p[1]][0])
+            else:
+                need(g.tensor, pe, ("y", s, 0))
             need(g.tensor, pe, ("tiles", q, _chunk_of(q, s)))
-            need(g.tensor, pe, ("y", s, 0) if s else ("tiles", 0, 0))
             rhs = Y[:, TK * s:TK * (s + 1)] if s else W[:, 0:TK]
-            g.tensor.matmul(acc, W[:, o + TK + P * s:o + TK + P * (s + 1)], rhs, it[3], it[4]).then_inc(S["m%d" % q], 1)
-        else:
-            g.vector.wait_ge(S["m%d" % q], q)
-            need(g.vector, ve, ("b", q, 0))
-            g.vector.tensor_tensor(Y[:, TK * q:TK * (q + 1)], W[:, o:o + TK], acc,
-                                   AluOpType.subtract).then_inc(S["v%d" % q], 1)
+            g.tensor.matmul(acc, W[:, o + TK + P * s:o + TK + P * (s + 1)], rhs, s == 0, s == q - 1).then_inc(S["m%d" % q], 1)
+            if s == q - 1:
+                g.vector.wait_ge(S["m%d" % q], q)
+                need(g.vector, ve, ("b", q, 0))
+                g.vector.tensor_tensor(Y[:, TK * q:TK * (q + 1)], W[:, o:o + TK], acc,
+                                       AluOpType.subtract).then_inc(S["v%d" % q], 1)
 
-    g.sync.wait_ge(S["v%d" % rank], 1)
-    g.sync.dma_start(T.y[:], Y[:, TK * rank:TK * (rank + 1)]).then_inc(S.st, 16)
-    g.sync.wait_ge(S.st, 16)
+    if rank is not None:
+        g.sync.wait_ge(S["v%d" % rank], 1)
+        g.sync.dma_start(T.y[:], Y[:, TK * rank:TK * (rank + 1)]).then_inc(S.st, 16)
+        g.sync.wait_ge(S.st, 16)

from concourse.mybir import AluOpType

N, TK, P = 8, 64, 128
NL = 4


def _off(q):
    return TK * q + P * (q * (q - 1) // 2)


SCRATCH = {
    "w": ("sbuf", [P, _off(N)], "float32"),
    "yy": ("sbuf", [P, TK * N], "float32"),
}
for _q in range(1, N):
    SCRATCH["ps%d" % _q] = ("psum", [P, 512], "float32")

TILES = {0: [0], 1: [0, 1], 2: [0, 2], 3: [0, 1, 2], 4: [0, 2, 1, 1], 5: [1, 1, 1, 1, 1], 6: [2, 1, 1, 1, 1], 7: [7]}
ENTRY = [5]
LAUNCH = {4: ({0: 0, 1: 0, 2: 0, 3: 0}, [5]), 5: ({3: 0, 4: 0}, None), 6: ({2: 0, 3: 1, 4: 0}, None)}
PIECES = {7: [(1, 1), (2, 2), (3, 3)], 6: [(1, 1), (2, 2), (3, 3)], 5: [(1, 2), (3, 3)], 4: [(1, 3)]}


def _chunks(q):
    out, a = [], _off(q)
    for k, n in enumerate(TILES[q]):
        z = a + P * n + (TK if k == 0 else 0)
        out.append((a, z))
        a = z
    return out


def _chunk_of(q, s):
    k = 0
    while s >= sum(TILES[q][:k + 1]):
        k += 1
    return k


_YS = sorted(set([p for u in PIECES for p in PIECES[u]] + [(q, q) for q in range(1, NL)]))
SEMAPHORES = (["r%d_%d" % (q, k) for q in range(N - 1) for k in range(len(_chunks(q)))] + ["y%d_%d" % p for p in _YS]
              + ["m%d" % q for q in range(1, N)] + ["v%d" % q for q in range(1, N)]
              + ["ld%d" % k for k in range(max(len(t) for t in TILES.values()))] + ["ldb", "st", "sent"])

_CACHE = {}


def _bits(m):
    return bin(m).count("1")


def _plan(T, topo):
    if "p" in _CACHE:
        return _CACHE["p"]
    cores = list(T.cores)
    world = range((max(topo.host(c) for c in cores) + 1) * topo.CORES_PER_HOST)
    rk = lambda c: topo.rack(topo.host(c))
    same_chip = lambda a, b: topo.host(a) == topo.host(b) and topo.chip(a) == topo.chip(b)
    low, up = list(range(NL)), list(range(NL, N))

    solver = {}
    for q in low:
        o = cores[q]
        if rk(o) == rk(cores[N - 1]):
            near = [cores[u] for u in up if rk(cores[u]) == rk(o)]
            cand = [c for c in world if same_chip(c, o) and c not in cores and all(topo.may_write(c, n) for n in near)]
            other = [c for c in cand if topo.die(c) != topo.die(o)]
            solver[q] = (other or cand)[0]
    sol = [solver[q] for q in sorted(solver)]
    serve = {}
    for u in up:
        ok = [s for s in sol if topo.may_write(s, cores[u])]
        home = [s for s in ok if topo.host(s) == topo.host(cores[u])]
        serve[u] = (home or ok)[0]

    hops = []
    for q in low:
        o = cores[q]
        for k in range(len(TILES[q])):
            for s in sol:
                if topo.may_write(o, s):
                    hops.append((q, k, o, s))
                else:
                    hops.append((q, k, [x for x in sol if topo.may_write(o, x) and topo.may_write(x, s)][0], s))
    first = [s for s in sol if topo.may_write(cores[0], s)][0]
    for u in up:
        hops.append((0, 0, first if topo.may_write(first, cores[u]) else serve[u], cores[u]))
    for q in low[1:]:
        if q not in solver:
            for p in range(q):
                for k in range(len(TILES[p])):
                    hops.append((p, k, cores[p], cores[q]))

    for q in up[:-1]:
        o = cores[q]
        direct = [c for c in cores[q + 1:] if topo.may_write(o, c)]
        turn, via = [], []
        if q in ENTRY:
            r = [h for h in direct for c in cores[q + 1:] if c not in direct and topo.may_write(h, c) and rk(h) == rk(c)][0]
            via = [c for c in cores[q + 1:] if rk(c) == rk(r)]
            cand = [c for c in world if same_chip(c, r) and c not in cores and topo.may_write(o, c)
                    and all(topo.may_write(c, v) for v in via)]
            here = [c for c in cand if topo.die(c) == topo.die(r)]
            there = [c for c in cand if topo.die(c) != topo.die(r)]
            turn = [here[0]] + [there[(k + 1) % 2] for k in range(1, len(TILES[q]))]
        for k in range(len(TILES[q])):
            used = []
            for c in cores[q + 1:]:
                if c in via:
                    relay = turn[k]
                elif c in direct:
                    hops.append((q, k, o, c))
                    continue
                else:
                    relay = [h for h in direct if topo.may_write(h, c) and rk(h) == rk(c)][0]
                hops.append((q, k, relay, c))
                if relay not in cores and relay not in used:
                    used.append(relay)
            for h in used:
                hops.append((q, k, o, h))

    busy = set(c for h in hops for c in h[2:])
    for q in sorted(LAUNCH):
        o = cores[q]
        which, only = LAUNCH[q]
        free = [c for c in world if same_chip(c, o) and c not in cores and c not in busy and topo.die(c) == topo.die(o)]
        free.reverse()
        handed = []
        for i, h in enumerate(hops):
            if h[0] == q and h[2] == o and h[1] in which and (only is None or h[3] in [cores[u] for u in only]):
                lc = free[which[h[1]]]
                hops[i] = (q, h[1], lc, h[3])
                if (h[1], lc) not in handed:
                    handed.append((h[1], lc))
        for (k, lc) in handed:
            hops.append((q, k, o, lc))

    ys = {}
    for q in solver:
        mine = sorted([u for u in up if serve[u] == solver[q]], reverse=True)
        items = sorted((hi, i, lo, cores[u]) for i, u in enumerate(mine) for (lo, hi) in PIECES[u])
        ys[solver[q]] = [(lo, hi, d) for (hi, i, lo, d) in items] + [(q, q, cores[q])]

    onward = lambda h: len([1 for x in hops if x[:2] == h[:2] and x[2] == h[3]])
    rank_of = lambda c: cores.index(c) if c in cores else -1
    sends, cnt = {}, {}
    for s in sorted(set(h[2] for h in hops)):
        mine = [h for h in hops if h[2] == s]
        dsts = [h[3] for h in mine] + [d for (_, _, d) in ys.get(s, [])]
        off_chip = [topo.mask(s, d) for d in dsts if not same_chip(s, d)]
        own = [h for h in mine if cores[h[0]] == s]
        fwd = [h for h in mine if cores[h[0]] != s]
        own.sort(key=lambda h: (h[1], onward(h) == 0, same_chip(s, h[3]), -rank_of(h[3])))
        fwd.sort(key=lambda h: (h[3] not in sol, h[0], h[1], -rank_of(h[3])))
        out = []
        for (kind, a, b, d) in [("r", h[0], h[1], h[3]) for h in own + fwd] + [("y", lo, hi, d) for (lo, hi, d) in ys.get(s, [])]:
            m = topo.mask(s, d)
            if same_chip(s, d) and off_chip and (m & ~off_chip[0]):
                m = m & ~off_chip[0]
            out.append((kind, a, b, d, m))
            cnt[(d, "%s%d_%d" % (kind, a, b))] = _bits(m)
        sends[s] = out
    _CACHE["p"] = (sends, cnt, solver)
    return _CACHE["p"]


def rank_program(g, core, T, topo):
    sends, cnt, solver = _plan(T, topo)
    mine = sends.get(core, [])
    rank = T.rank_of(core)
    if rank is None and not mine:
        return
    S, W, Y = T.sem, T.w, T.yy

    if rank is not None:
        o = _off(rank)
        g.scalar.dma_start(W[:, o:o + TK], T.b[:]).then_inc(S.ldb, 16)
        for k, (a, z) in enumerate(_chunks(rank)):
            a = max(a, o + TK)
            if z > a:
                g.sync.dma_start(W[:, a:z], T.l[:, a - o - TK:z - o - TK]).then_inc(S["ld%d" % k], 16)
        if rank == 0:
            g.sync.dma_start(T.y[:], T.b[:]).then_inc(S.st, 16)
            g.sync.wait_ge(S.st, 16)

    total, seen = 0, set()
    for (kind, a, b, dst, mask) in mine:
        name = "%s%d_%d" % (kind, a, b)
        if kind == "y":
            for s in range(a, b + 1):
                if ("v", s) not in seen:
                    seen.add(("v", s))
                    g.wait_ge(S["v%d" % s], 1)
            buf, c0, c1 = Y, TK * a, TK * (b + 1)
        else:
            if name not in seen:
                seen.add(name)
                if a == rank:
                    if b == 0:
                        g.wait_ge(S.ldb, 16)
                    if TILES[a][b]:
                        g.wait_ge(S["ld%d" % b], 16)
                else:
                    g.wait_ge(S[name], cnt[(core, name)])
            buf = W
            c0, c1 = _chunks(a)[b]
        rid, pid = topo.addr(dst, core)
        g.remote_dma(out_ap=buf[:, c0:c1], in_ap=buf[:, c0:c1], remote_sem=S[name], local_sem=S.sent, pid=pid,
                     routing_id=rid, dma_engine_mask=mask)
        total += _bits(mask)
    if total:
        g.wait_ge(S.sent, total)

    if core in solver.values():
        lo, hi, pieces = 1, NL - 1, []
    elif not rank:
        return
    elif rank in solver:
        name = "y%d_%d" % (rank, rank)
        g.sync.wait_ge(S[name], cnt[(core, name)])
        g.sync.dma_start(T.y[:], Y[:, TK * rank:TK * (rank + 1)]).then_inc(S.st, 16)
        g.sync.wait_ge(S.st, 16)
        return
    elif rank < NL:
        lo, hi, pieces = 1, rank, []
    else:
        lo, hi, pieces = NL, rank, PIECES[rank]

    pe, ve = set(), set()

    def need(queue, seen_set, key):
        if key in seen_set:
            return
        seen_set.add(key)
        kind, q, k = key
        if kind == "y":
            queue.wait_ge(S["v%d" % q], 1)
        elif kind == "p":
            queue.wait_ge(S["y%d_%d" % (q, k)], cnt[(core, "y%d_%d" % (q, k))])
        elif q != rank:
            queue.wait_ge(S["r%d_%d" % (q, k)], cnt[(core, "r%d_%d" % (q, k))])
        else:
            queue.wait_ge(S["ld%d" % k] if kind == "tiles" else S.ldb, 16)

    for s in range(hi):
        for q in range(max(lo, s + 1), hi + 1):
            o = _off(q)
            acc = T["ps%d" % q][:, 0:TK]
            if s == 0:
                need(g.tensor, pe, ("tiles", 0, 0))
            elif s < lo:
                need(g.tensor, pe, ("p",) + [p for p in pieces if p[0] <= s <= p[1]][0])
            else:
                need(g.tensor, pe, ("y", s, 0))
            need(g.tensor, pe, ("tiles", q, _chunk_of(q, s)))
            rhs = Y[:, TK * s:TK * (s + 1)] if s else W[:, 0:TK]
            g.tensor.matmul(acc, W[:, o + TK + P * s:o + TK + P * (s + 1)], rhs, s == 0, s == q - 1).then_inc(S["m%d" % q], 1)
            if s == q - 1:
                g.vector.wait_ge(S["m%d" % q], q)
                need(g.vector, ve, ("b", q, 0))
                g.vector.tensor_tensor(Y[:, TK * q:TK * (q + 1)], W[:, o:o + TK], acc,
                                       AluOpType.subtract).then_inc(S["v%d" % q], 1)

    if rank is not None:
        g.sync.wait_ge(S["v%d" % rank], 1)
        g.sync.dma_start(T.y[:], Y[:, TK * rank:TK * (rank + 1)]).then_inc(S.st, 16)
        g.sync.wait_ge(S.st, 16)
